import numpy as np
import ml_dtypes


def mxq(x, axis, fmt="e4m3"):
    dtype, down = {"e4m3": (ml_dtypes.float8_e4m3fn, 7), "e5m2": (ml_dtypes.float8_e5m2, 14)}[fmt]
    v = np.moveaxis(np.asarray(x, np.float32).astype(ml_dtypes.bfloat16).astype(np.float64), axis, -1)
    blocks = v.reshape(v.shape[:-1] + (-1, 32))
    amax = np.abs(blocks).max(-1, keepdims=True)
    byte = np.maximum(np.where(amax > 0, np.frexp(amax)[1] - 1 + 127, 0) - down, 1)
    scale = np.exp2(byte - 127.0)
    codes = (blocks / scale).astype(np.float32).astype(dtype).astype(np.float64)
    return np.moveaxis((codes * scale).reshape(v.shape), -1, axis)


WIDE = False


def mx_kscale(k):
    if not WIDE:
        return np.ones(k)
    levels = np.array([10, -10, 5, -5, 0])
    if k % 512:
        return np.exp2(np.random.permutation(np.resize(levels, k // 32))).repeat(32)
    a = np.empty((k // 512, 16))
    for p in range(k // 512):
        a[p, :8] = np.random.permutation(np.resize(levels, 8))
        for g in range(8):
            far = levels[np.abs(levels - a[p, g]) >= 10]
            a[p, g + 8] = far[np.random.randint(len(far))]
    return np.exp2(a.ravel()).repeat(32)


def f64(x):
    return np.asarray(x).astype(np.float64)


def striped(idx):
    return np.tile(idx.reshape(-1, 16).T, (8, 1)).astype(np.uint16)


def unstriped(offs):
    return offs[:16].T.reshape(-1).astype(np.int64)


def gelu(v):
    return 0.5 * v * (1.0 + np.tanh(np.sqrt(2.0 / np.pi) * (v + 0.044715 * v**3)))


K, T, E, C, H, N = 1024, 512, 4, 128, 512, 256


def by_expert(wq, xq):
    return np.concatenate([wq[e].T @ xq[:, e * C:(e + 1) * C] for e in range(E)], axis=1)


def setup_inputs():
    n = np.random.standard_normal
    s = mx_kscale(K)[:, None]
    u = mx_kscale(H)
    return {
        "xT": (n((K, T)) * s).astype(np.float32),
        "w1": (n((E, K, H)) / np.sqrt(K) / s[None]).astype(np.float32),
        "w3": (n((E, K, H)) / np.sqrt(K) / s[None] * u[None, None, :]).astype(np.float32),
        "w2": (n((E, H, N)) / np.sqrt(H) / u[None, :, None]).astype(np.float32),
        "gate": np.tile(np.random.uniform(0.2, 1.0, E * C), (N, 1)).astype(np.float32),
        "offs": striped(np.random.permutation(T)[:E * C]),
    }


def reference(xT, w1, w3, w2, gate, offs):
    idx = unstriped(offs)
    xq = mxq(f64(xT)[:, idx], 0, "e4m3")
    h = gelu(by_expert(mxq(f64(w1), 1, "e4m3"), xq))
    h = h * by_expert(mxq(f64(w3), 1, "e4m3"), xq)
    y = by_expert(mxq(f64(w2), 1, "e4m3"), mxq(h, 0, "e4m3"))
    out = np.zeros((N, T))
    out[:, idx] = f64(gate) * y
    return out

@@ -1,0 +1,290 @@
+from contextlib import ExitStack
+
+import concourse.mybir as mybir
+
+K, T, E, C, H, N = 1024, 512, 4, 128, 512, 256
+FLOPS = 2 * E * C * (2 * K * H + H * N)
+
+F32 = mybir.dt.float32
+BF16 = mybir.dt.bfloat16
+U32 = mybir.dt.uint32
+U16 = mybir.dt.uint16
+U8 = mybir.dt.uint8
+FP8X4 = mybir.dt.float8_e4m3fn_x4
+GELU = mybir.ActivationFunctionType.Gelu_apprx_tanh
+MULT = mybir.AluOpType.mult
+
+P = 128
+PACK = 4
+K_PASS = P * PACK
+PASSES = K // K_PASS
+NT = N // P
+HALF = 256
+RAW_BUFS = 10
+AHEAD = 8
+
+VECTOR_UNITS = [("w3", 0, 1), ("w3", 1, 1), ("w3", 2, 1), ("w3", 3, 1), ("w3", 3, 0), ("w2", 0, 0), ("w2", 1, 0), ("w2", 2, 0)]
+TOKEN_COPY_ON_VECTOR = [False, True]
+
+
+def tile_routed_moe_kernel(tc, xT, w1, w3, w2, gate, offs, out):
+    nc = tc.nc
+    with ExitStack() as ctx:
+        lists = ctx.enter_context(tc.tile_pool(name="lists", bufs=1))
+        keep = ctx.enter_context(tc.tile_pool(name="keep", bufs=1))
+        rawp = ctx.enter_context(tc.tile_pool(name="rawp", bufs=RAW_BUFS))
+        raw2p = ctx.enter_context(tc.tile_pool(name="raw2p", bufs=2))
+        stage = ctx.enter_context(tc.tile_pool(name="stage", bufs=3))
+        tokp = ctx.enter_context(tc.tile_pool(name="tokp", bufs=4))
+        work = ctx.enter_context(tc.tile_pool(name="work", bufs=2))
+        psum = ctx.enter_context(tc.psum_pool(name="psum", bufs=2))
+
+        offsets = lists.tile([P, T // 16], U16, name="offsets")
+        x_view = xT.rearrange("(g p t) n -> g p t n", p=P, t=PACK)
+
+        planes = {}
+        gates = []
+        raws = {}
+
+        arrivals = [("offs", 0, 0)]
+        arrivals += [("plane", 0, t) for t in range(PACK)] + [("w1", 0, 0)]
+        arrivals += [("plane", 1, t) for t in range(PACK)] + [("w1", 0, 1), ("w3", 0, 0), ("gate", 0, 0), ("w2", 0, 0), ("w3", 0, 1)]
+        for e in range(1, E - 1):
+            arrivals += [("w1", e, 0), ("w1", e, 1), ("w3", e, 0), ("w2", e, 0), ("w3", e, 1)]
+        arrivals += [("w1", E - 1, 0), ("w1", E - 1, 1), ("w3", E - 1, 0), ("w3", E - 1, 1), ("w2", E - 1, 0)]
+
+        def load(item):
+            kind, e, g = item
+            if kind == "offs":
+                nc.sync.dma_start(offsets[:], offs)
+            elif kind == "plane":
+                plane = keep.tile([P, T], F32, name="plane%d%d" % (e, g))
+                nc.sync.dma_start(plane[:], x_view[e, :, g, :])
+                planes[(e, g)] = plane
+            elif kind == "gate":
+                for nt in range(NT):
+                    gt = keep.tile([P, T], F32, name="gate%d" % nt)
+                    nc.sync.dma_start(gt[:], gate[nt * P:(nt + 1) * P, :])
+                    gates.append(gt)
+            elif kind == "w2":
+                raw2 = raw2p.tile([P, PACK, N], F32, name="raw2")
+                nc.sync.dma_start(raw2[:], w2[e].rearrange("(p j) n -> p j n", j=PACK))
+                raws[item] = raw2
+            else:
+                src = w1 if kind == "w1" else w3
+                raw = rawp.tile([P, PACK, H], F32, name="raw")
+                nc.sync.dma_start(raw[:], src[e, g * K_PASS:(g + 1) * K_PASS, :].rearrange("(p j) c -> p j c", j=PACK))
+                raws[item] = raw
+
+        progress = {"next": 0, "weights": 0}
+
+        def load_until(wanted):
+            while progress["next"] < len(arrivals) and progress["weights"] < wanted:
+                item = arrivals[progress["next"]]
+                load(item)
+                progress["next"] += 1
+                if item[0] in ("w1", "w3", "w2"):
+                    progress["weights"] += 1
+
+        load_until(AHEAD)
+
+        zero = keep.tile([P, 1], F32, name="zero")
+        warm = keep.tile([P, 1], F32, name="warm")
+        nc.vector.memset(zero[:], 0.0)
+        nc.scalar.activation(warm[:], zero[:], GELU)
+
+        gathered = {}
+        grouped = {}
+        codes = {}
+        copied = {"n": 0}
+
+        def gather(g, t, half):
+            if (g, half) not in gathered:
+                gathered[(g, half)] = tokp.tile([P, PACK, HALF], F32, name="g4")
+            cols = offsets[:, half * (HALF // 16):(half + 1) * (HALF // 16)]
+            nc.vector.tensor_copy(gathered[(g, half)][:, t, :], planes[(g, t)][:].indirect(cols))
+
+        def engine_copy(on_vector, dst, src):
+            if on_vector:
+                nc.vector.tensor_copy(out=dst, in_=src)
+            else:
+                nc.scalar.copy(out=dst, in_=src)
+
+        def token_copy(g, half):
+            xg = tokp.tile([P, HALF * PACK], BF16, name="xg", align_bytes=64)
+            engine_copy(
+                TOKEN_COPY_ON_VECTOR[g],
+                xg[:].rearrange("p (c i j) -> p c j i", i=4, j=PACK),
+                gathered[(g, half)][:].rearrange("p j (c i) -> p c j i", i=4),
+            )
+            grouped[("x", g, half)] = xg
+
+        def quantise(item, width):
+            kind, e, g = item
+            cd = keep.tile([P, width], U32, name="%sq%d%d" % (kind, e, g), align_bytes=64)
+            sc = keep.tile([P, width], U8, name="%ss%d%d" % (kind, e, g), align_bytes=64)
+            nc.vector.quantize_mx(out=cd[:].bitcast(FP8X4), scales=sc[:], in_=grouped[item][:])
+            codes[item] = (cd, sc)
+
+        def weight_copy(item):
+            kind, e, g = item
+            raw = raws[item]
+            if kind == "w2":
+                wg = stage.tile([P, N * PACK], BF16, name="w2g", align_bytes=64)
+                dst = wg[:].rearrange("p (c i j) -> p c j i", i=4, j=PACK)
+                src = raw[:].rearrange("p j (c i) -> p c j i", i=4)
+            else:
+                wg = stage.tile([P, H * PACK], BF16, name="wg", align_bytes=64)
+                dst = wg[:].rearrange("p (t m j) -> p m j t", t=PACK, j=PACK)
+                src = raw[:].rearrange("p j (m t) -> p m j t", t=PACK)
+            engine_copy(item in VECTOR_UNITS, dst, src)
+            grouped[item] = wg
+            copied["n"] += 1
+            load_until(AHEAD + copied["n"])
+
+        accs = {}
+
+        def first_layer(kind, e):
+            acc = psum.tile([P, PACK, C], F32, name="acc_" + kind)
+            for t in range(PACK):
+                for g in range(PASSES):
+                    wc, ws = codes[(kind, e, g)]
+                    xc, xs = codes[("x", g, e // 2)]
+                    sl = slice((e % 2) * C, (e % 2 + 1) * C)
+                    nc.tensor.matmul_mx(
+                        out=acc[:, t, :],
+                        lhsT=wc[:, t * P:(t + 1) * P].bitcast(FP8X4),
+                        lhsT_scale=ws[:, t * P:(t + 1) * P],
+                        rhs=xc[:, sl].bitcast(FP8X4),
+                        rhs_scale=xs[:, sl],
+                        start=(g == 0),
+                        stop=(g == PASSES - 1),
+                    )
+            accs[(kind, e)] = acc
+
+        def gelu(e):
+            ga = work.tile([P, PACK, C], F32, name="ga")
+            nc.scalar.activation(ga[:], accs[("w1", e)][:], GELU)
+            accs[("ga", e)] = ga
+
+        def hidden(e):
+            hb = work.tile([P, C * PACK], BF16, name="hb", align_bytes=64)
+            nc.vector.tensor_tensor(
+                out=hb[:].rearrange("p (n t) -> p n t", t=PACK),
+                in0=accs[("ga", e)][:].rearrange("p t n -> p n t"),
+                in1=accs[("w3", e)][:].rearrange("p t n -> p n t"),
+                op=MULT,
+            )
+            accs[("hb", e)] = hb
+
+        def hidden_quantise(e):
+            hq = work.tile([P, C], U32, name="hq", align_bytes=64)
+            hs = work.tile([P, C], U8, name="hs", align_bytes=64)
+            nc.vector.quantize_mx(out=hq[:].bitcast(FP8X4), scales=hs[:], in_=accs[("hb", e)][:])
+            wc, ws = codes[("w2", e, 0)]
+            acc_y = psum.tile([P, NT, C], F32, name="acc_y")
+            for nt in range(NT):
+                nc.tensor.matmul_mx(
+                    out=acc_y[:, nt, :],
+                    lhsT=wc[:, nt * P:(nt + 1) * P].bitcast(FP8X4),
+                    lhsT_scale=ws[:, nt * P:(nt + 1) * P],
+                    rhs=hq[:].bitcast(FP8X4),
+                    rhs_scale=hs[:],
+                    start=True,
+                    stop=True,
+                )
+            accs[("y", e)] = acc_y
+
+        def leave_psum(e):
+            ysb = work.tile([P, NT, C], F32, name="ysb")
+            nc.scalar.copy(out=ysb[:], in_=accs[("y", e)][:])
+            accs[("ysb", e)] = ysb
+
+        windows = [keep.tile([P, T], F32, name="window%d" % nt) for nt in range(NT)]
+
+        def scatter(e, nt):
+            nc.vector.tensor_tensor(
+                windows[nt][:].indirect(offsets[:, e * (C // 16):(e + 1) * (C // 16)]),
+                accs[("ysb", e)][:, nt, :],
+                gates[nt][:, e * C:(e + 1) * C],
+                MULT,
+            )
+
+        for t in range(PACK):
+            gather(0, t, 0)
+            gather(0, t, 1)
+        weight_copy(("w1", 0, 0))
+        token_copy(0, 0)
+        token_copy(0, 1)
+        for t in range(PACK):
+            gather(1, t, 0)
+            gather(1, t, 1)
+        quantise(("x", 0, 0), HALF)
+        quantise(("x", 0, 1), HALF)
+        weight_copy(("w1", 0, 1))
+        token_copy(1, 0)
+        token_copy(1, 1)
+
+        last = E - 1
+        for e in range(E):
+            if e > 0:
+                weight_copy(("w1", e, 0))
+                if e > 1:
+                    scatter(e - 2, 0)
+                    scatter(e - 2, 1)
+                hidden(e - 1)
+                weight_copy(("w1", e, 1))
+            quantise(("w1", e, 0), H)
+            if e > 0:
+                hidden_quantise(e - 1)
+            weight_copy(("w3", e, 0))
+            if e > 0:
+                leave_psum(e - 1)
+            if e == 0:
+                quantise(("x", 1, 0), HALF)
+                quantise(("x", 1, 1), HALF)
+            quantise(("w1", e, 1), H)
+            first_layer("w1", e)
+            if e < last:
+                weight_copy(("w2", e, 0))
+            gelu(e)
+            quantise(("w3", e, 0), H)
+            weight_copy(("w3", e, 1))
+            if e < last:
+                quantise(("w2", e, 0), N)
+            else:
+                weight_copy(("w2", e, 0))
+            quantise(("w3", e, 1), H)
+            first_layer("w3", e)
+
+        scatter(last - 1, 0)
+        quantise(("w2", last, 0), N)
+        hidden(last)
+        hq = work.tile([P, C], U32, name="hq", align_bytes=64)
+        hs = work.tile([P, C], U8, name="hs", align_bytes=64)
+        nc.vector.quantize_mx(out=hq[:].bitcast(FP8X4), scales=hs[:], in_=accs[("hb", last)][:])
+        wc, ws = codes[("w2", last, 0)]
+        y_last = []
+        for nt in range(NT):
+            acc_y = psum.tile([P, C], F32, name="acc_y")
+            nc.tensor.matmul_mx(
+                out=acc_y[:],
+                lhsT=wc[:, nt * P:(nt + 1) * P].bitcast(FP8X4),
+                lhsT_scale=ws[:, nt * P:(nt + 1) * P],
+                rhs=hq[:].bitcast(FP8X4),
+                rhs_scale=hs[:],
+                start=True,
+                stop=True,
+            )
+            y_sb = keep.tile([P, C], F32, name="y_last%d" % nt)
+            nc.scalar.copy(out=y_sb[:], in_=acc_y[:])
+            y_last.append(y_sb)
+        scatter(last - 1, 1)
+        for nt in range(NT):
+            nc.vector.tensor_tensor(
+                windows[nt][:].indirect(offsets[:, last * (C // 16):(last + 1) * (C // 16)]),
+                y_last[nt][:],
+                gates[nt][:, last * C:(last + 1) * C],
+                MULT,
+            )
+            nc.sync.dma_start(out[nt * P:(nt + 1) * P, :], windows[nt][:])

@@ -23,7 +23,7 @@ HALF = 256
 RAW_BUFS = 10
 AHEAD = 8
 
-VECTOR_UNITS = [("w3", 0, 1), ("w3", 1, 1), ("w3", 2, 1), ("w3", 3, 1), ("w3", 3, 0), ("w2", 0, 0), ("w2", 1, 0), ("w2", 2, 0)]
+VECTOR_UNITS = [("w1", 0, 1), ("w1", 1, 1), ("w1", 2, 1), ("w1", 3, 1), ("w3", 0, 1), ("w3", 1, 1), ("w3", 2, 1), ("w3", 3, 1)]
 TOKEN_COPY_ON_VECTOR = [False, True]
 
 
@@ -229,22 +229,20 @@ def tile_routed_moe_kernel(tc, xT, w1, w3, w2, gate, offs, out):
         for e in range(E):
             if e > 0:
                 weight_copy(("w1", e, 0))
-                if e > 1:
-                    scatter(e - 2, 0)
-                    scatter(e - 2, 1)
                 hidden(e - 1)
-                weight_copy(("w1", e, 1))
-            quantise(("w1", e, 0), H)
-            if e > 0:
                 hidden_quantise(e - 1)
-            weight_copy(("w3", e, 0))
-            if e > 0:
+                weight_copy(("w1", e, 1))
                 leave_psum(e - 1)
+            quantise(("w1", e, 0), H)
+            weight_copy(("w3", e, 0))
             if e == 0:
                 quantise(("x", 1, 0), HALF)
                 quantise(("x", 1, 1), HALF)
             quantise(("w1", e, 1), H)
             first_layer("w1", e)
+            if e > 0:
+                scatter(e - 1, 0)
+                scatter(e - 1, 1)
             if e < last:
                 weight_copy(("w2", e, 0))
             gelu(e)
@@ -257,7 +255,6 @@ def tile_routed_moe_kernel(tc, xT, w1, w3, w2, gate, offs, out):
             quantise(("w3", e, 1), H)
             first_layer("w3", e)
 
-        scatter(last - 1, 0)
         quantise(("w2", last, 0), N)
         hidden(last)
         hq = work.tile([P, C], U32, name="hq", align_bytes=64)
@@ -279,7 +276,6 @@ def tile_routed_moe_kernel(tc, xT, w1, w3, w2, gate, offs, out):
             y_sb = keep.tile([P, C], F32, name="y_last%d" % nt)
             nc.scalar.copy(out=y_sb[:], in_=acc_y[:])
             y_last.append(y_sb)
-        scatter(last - 1, 1)
         for nt in range(NT):
             nc.vector.tensor_tensor(
                 windows[nt][:].indirect(offsets[:, last * (C // 16):(last + 1) * (C // 16)]),

@@ -36,6 +36,7 @@ def tile_routed_moe_kernel(tc, xT, w1, w3, w2, gate, offs, out):
         raw2p = ctx.enter_context(tc.tile_pool(name="raw2p", bufs=2))
         stage = ctx.enter_context(tc.tile_pool(name="stage", bufs=3))
         tokp = ctx.enter_context(tc.tile_pool(name="tokp", bufs=4))
+        gatp = ctx.enter_context(tc.tile_pool(name="gatp", bufs=2))
         work = ctx.enter_context(tc.tile_pool(name="work", bufs=2))
         psum = ctx.enter_context(tc.psum_pool(name="psum", bufs=2))
 
@@ -100,7 +101,7 @@ def tile_routed_moe_kernel(tc, xT, w1, w3, w2, gate, offs, out):
 
         def gather(g, t, half):
             if (g, half) not in gathered:
-                gathered[(g, half)] = tokp.tile([P, PACK, HALF], F32, name="g4")
+                gathered[(g, half)] = gatp.tile([P, PACK, HALF], F32, name="g4")
             cols = offsets[:, half * (HALF // 16):(half + 1) * (HALF // 16)]
             nc.vector.tensor_copy(gathered[(g, half)][:, t, :], planes[(g, t)][:].indirect(cols))
 
@@ -210,20 +211,22 @@ def tile_routed_moe_kernel(tc, xT, w1, w3, w2, gate, offs, out):
                 MULT,
             )
 
-        for t in range(PACK):
-            gather(0, t, 0)
-            gather(0, t, 1)
+        for g in range(PASSES):
+            for t in range(PACK):
+                gather(g, t, 0)
         weight_copy(("w1", 0, 0))
         token_copy(0, 0)
-        token_copy(0, 1)
-        for t in range(PACK):
-            gather(1, t, 0)
-            gather(1, t, 1)
-        quantise(("x", 0, 0), HALF)
-        quantise(("x", 0, 1), HALF)
-        weight_copy(("w1", 0, 1))
         token_copy(1, 0)
+        quantise(("x", 0, 0), HALF)
+        quantise(("x", 1, 0), HALF)
+        weight_copy(("w1", 0, 1))
+        for g in range(PASSES):
+            for t in range(PACK):
+                gather(g, t, 1)
+        token_copy(0, 1)
         token_copy(1, 1)
+        quantise(("x", 0, 1), HALF)
+        quantise(("x", 1, 1), HALF)
 
         last = E - 1
         for e in range(E):
@@ -235,9 +238,6 @@ def tile_routed_moe_kernel(tc, xT, w1, w3, w2, gate, offs, out):
                 leave_psum(e - 1)
             quantise(("w1", e, 0), H)
             weight_copy(("w3", e, 0))
-            if e == 0:
-                quantise(("x", 1, 0), HALF)
-                quantise(("x", 1, 1), HALF)
             quantise(("w1", e, 1), H)
             first_layer("w1", e)
             if e > 0:

@@ -23,7 +23,7 @@ HALF = 256
 RAW_BUFS = 10
 AHEAD = 8
 
-VECTOR_UNITS = [("w1", 0, 1), ("w1", 1, 1), ("w1", 2, 1), ("w1", 3, 1), ("w3", 0, 1), ("w3", 1, 1), ("w3", 2, 1), ("w3", 3, 1)]
+VECTOR_UNITS = [("w1", 0, 1), ("w1", 1, 1), ("w1", 2, 1), ("w1", 3, 1), ("w3", 0, 1), ("w3", 1, 1), ("w3", 2, 1), ("w3", 3, 1), ("w2", 0, 0), ("w2", 1, 0), ("w2", 2, 0)]
 TOKEN_COPY_ON_VECTOR = [False, True]
 
 
@@ -36,7 +36,6 @@ def tile_routed_moe_kernel(tc, xT, w1, w3, w2, gate, offs, out):
         raw2p = ctx.enter_context(tc.tile_pool(name="raw2p", bufs=2))
         stage = ctx.enter_context(tc.tile_pool(name="stage", bufs=3))
         tokp = ctx.enter_context(tc.tile_pool(name="tokp", bufs=4))
-        gatp = ctx.enter_context(tc.tile_pool(name="gatp", bufs=2))
         work = ctx.enter_context(tc.tile_pool(name="work", bufs=2))
         psum = ctx.enter_context(tc.psum_pool(name="psum", bufs=2))
 
@@ -101,7 +100,7 @@ def tile_routed_moe_kernel(tc, xT, w1, w3, w2, gate, offs, out):
 
         def gather(g, t, half):
             if (g, half) not in gathered:
-                gathered[(g, half)] = gatp.tile([P, PACK, HALF], F32, name="g4")
+                gathered[(g, half)] = tokp.tile([P, PACK, HALF], F32, name="g4")
             cols = offsets[:, half * (HALF // 16):(half + 1) * (HALF // 16)]
             nc.vector.tensor_copy(gathered[(g, half)][:, t, :], planes[(g, t)][:].indirect(cols))
 
@@ -211,22 +210,20 @@ def tile_routed_moe_kernel(tc, xT, w1, w3, w2, gate, offs, out):
                 MULT,
             )
 
-        for g in range(PASSES):
-            for t in range(PACK):
-                gather(g, t, 0)
+        for t in range(PACK):
+            gather(0, t, 0)
+            gather(0, t, 1)
         weight_copy(("w1", 0, 0))
         token_copy(0, 0)
-        token_copy(1, 0)
-        quantise(("x", 0, 0), HALF)
-        quantise(("x", 1, 0), HALF)
-        weight_copy(("w1", 0, 1))
-        for g in range(PASSES):
-            for t in range(PACK):
-                gather(g, t, 1)
         token_copy(0, 1)
-        token_copy(1, 1)
+        for t in range(PACK):
+            gather(1, t, 0)
+            gather(1, t, 1)
+        quantise(("x", 0, 0), HALF)
         quantise(("x", 0, 1), HALF)
-        quantise(("x", 1, 1), HALF)
+        weight_copy(("w1", 0, 1))
+        token_copy(1, 0)
+        token_copy(1, 1)
 
         last = E - 1
         for e in range(E):
@@ -238,6 +235,9 @@ def tile_routed_moe_kernel(tc, xT, w1, w3, w2, gate, offs, out):
                 leave_psum(e - 1)
             quantise(("w1", e, 0), H)
             weight_copy(("w3", e, 0))
+            if e == 0:
+                quantise(("x", 1, 0), HALF)
+                quantise(("x", 1, 1), HALF)
             quantise(("w1", e, 1), H)
             first_layer("w1", e)
             if e > 0:

@@ -24,7 +24,7 @@ RAW_BUFS = 10
 AHEAD = 8
 
 VECTOR_UNITS = [("w1", 0, 1), ("w1", 1, 1), ("w1", 2, 1), ("w1", 3, 1), ("w3", 0, 1), ("w3", 1, 1), ("w3", 2, 1), ("w3", 3, 1), ("w2", 0, 0), ("w2", 1, 0), ("w2", 2, 0)]
-TOKEN_COPY_ON_VECTOR = [False, True]
+TOKEN_COPY_ON_VECTOR = [True, True]
 
 
 def tile_routed_moe_kernel(tc, xT, w1, w3, w2, gate, offs, out):

from contextlib import ExitStack

import concourse.mybir as mybir

K, T, E, C, H, N = 1024, 512, 4, 128, 512, 256
FLOPS = 2 * E * C * (2 * K * H + H * N)

F32 = mybir.dt.float32
BF16 = mybir.dt.bfloat16
U32 = mybir.dt.uint32
U16 = mybir.dt.uint16
U8 = mybir.dt.uint8
FP8X4 = mybir.dt.float8_e4m3fn_x4
GELU = mybir.ActivationFunctionType.Gelu_apprx_tanh
MULT = mybir.AluOpType.mult

P = 128
PACK = 4
K_PASS = P * PACK
PASSES = K // K_PASS
NT = N // P
HALF = 256
RAW_BUFS = 10
AHEAD = 8

VECTOR_UNITS = [("w1", 0, 1), ("w1", 1, 1), ("w1", 2, 1), ("w1", 3, 1), ("w3", 0, 1), ("w3", 1, 1), ("w3", 2, 1), ("w3", 3, 1), ("w2", 0, 0), ("w2", 1, 0), ("w2", 2, 0)]
TOKEN_COPY_ON_VECTOR = [True, True]


def tile_routed_moe_kernel(tc, xT, w1, w3, w2, gate, offs, out):
    nc = tc.nc
    with ExitStack() as ctx:
        lists = ctx.enter_context(tc.tile_pool(name="lists", bufs=1))
        keep = ctx.enter_context(tc.tile_pool(name="keep", bufs=1))
        rawp = ctx.enter_context(tc.tile_pool(name="rawp", bufs=RAW_BUFS))
        raw2p = ctx.enter_context(tc.tile_pool(name="raw2p", bufs=2))
        stage = ctx.enter_context(tc.tile_pool(name="stage", bufs=3))
        tokp = ctx.enter_context(tc.tile_pool(name="tokp", bufs=4))
        work = ctx.enter_context(tc.tile_pool(name="work", bufs=2))
        psum = ctx.enter_context(tc.psum_pool(name="psum", bufs=2))

        offsets = lists.tile([P, T // 16], U16, name="offsets")
        x_view = xT.rearrange("(g p t) n -> g p t n", p=P, t=PACK)

        planes = {}
        gates = []
        raws = {}

        arrivals = [("offs", 0, 0)]
        arrivals += [("plane", 0, t) for t in range(PACK)] + [("w1", 0, 0)]
        arrivals += [("plane", 1, t) for t in range(PACK)] + [("w1", 0, 1), ("w3", 0, 0), ("gate", 0, 0), ("w2", 0, 0), ("w3", 0, 1)]
        for e in range(1, E - 1):
            arrivals += [("w1", e, 0), ("w1", e, 1), ("w3", e, 0), ("w2", e, 0), ("w3", e, 1)]
        arrivals += [("w1", E - 1, 0), ("w1", E - 1, 1), ("w3", E - 1, 0), ("w3", E - 1, 1), ("w2", E - 1, 0)]

        def load(item):
            kind, e, g = item
            if kind == "offs":
                nc.sync.dma_start(offsets[:], offs)
            elif kind == "plane":
                plane = keep.tile([P, T], F32, name="plane%d%d" % (e, g))
                nc.sync.dma_start(plane[:], x_view[e, :, g, :])
                planes[(e, g)] = plane
            elif kind == "gate":
                for nt in range(NT):
                    gt = keep.tile([P, T], F32, name="gate%d" % nt)
                    nc.sync.dma_start(gt[:], gate[nt * P:(nt + 1) * P, :])
                    gates.append(gt)
            elif kind == "w2":
                raw2 = raw2p.tile([P, PACK, N], F32, name="raw2")
                nc.sync.dma_start(raw2[:], w2[e].rearrange("(p j) n -> p j n", j=PACK))
                raws[item] = raw2
            else:
                src = w1 if kind == "w1" else w3
                raw = rawp.tile([P, PACK, H], F32, name="raw")
                nc.sync.dma_start(raw[:], src[e, g * K_PASS:(g + 1) * K_PASS, :].rearrange("(p j) c -> p j c", j=PACK))
                raws[item] = raw

        progress = {"next": 0, "weights": 0}

        def load_until(wanted):
            while progress["next"] < len(arrivals) and progress["weights"] < wanted:
                item = arrivals[progress["next"]]
                load(item)
                progress["next"] += 1
                if item[0] in ("w1", "w3", "w2"):
                    progress["weights"] += 1

        load_until(AHEAD)

        zero = keep.tile([P, 1], F32, name="zero")
        warm = keep.tile([P, 1], F32, name="warm")
        nc.vector.memset(zero[:], 0.0)
        nc.scalar.activation(warm[:], zero[:], GELU)

        gathered = {}
        grouped = {}
        codes = {}
        copied = {"n": 0}

        def gather(g, t, half):
            if (g, half) not in gathered:
                gathered[(g, half)] = tokp.tile([P, PACK, HALF], F32, name="g4")
            cols = offsets[:, half * (HALF // 16):(half + 1) * (HALF // 16)]
            nc.vector.tensor_copy(gathered[(g, half)][:, t, :], planes[(g, t)][:].indirect(cols))

        def engine_copy(on_vector, dst, src):
            if on_vector:
                nc.vector.tensor_copy(out=dst, in_=src)
            else:
                nc.scalar.copy(out=dst, in_=src)

        def token_copy(g, half):
            xg = tokp.tile([P, HALF * PACK], BF16, name="xg", align_bytes=64)
            engine_copy(
                TOKEN_COPY_ON_VECTOR[g],
                xg[:].rearrange("p (c i j) -> p c j i", i=4, j=PACK),
                gathered[(g, half)][:].rearrange("p j (c i) -> p c j i", i=4),
            )
            grouped[("x", g, half)] = xg

        def quantise(item, width):
            kind, e, g = item
            cd = keep.tile([P, width], U32, name="%sq%d%d" % (kind, e, g), align_bytes=64)
            sc = keep.tile([P, width], U8, name="%ss%d%d" % (kind, e, g), align_bytes=64)
            nc.vector.quantize_mx(out=cd[:].bitcast(FP8X4), scales=sc[:], in_=grouped[item][:])
            codes[item] = (cd, sc)

        def weight_copy(item):
            kind, e, g = item
            raw = raws[item]
            if kind == "w2":
                wg = stage.tile([P, N * PACK], BF16, name="w2g", align_bytes=64)
                dst = wg[:].rearrange("p (c i j) -> p c j i", i=4, j=PACK)
                src = raw[:].rearrange("p j (c i) -> p c j i", i=4)
            else:
                wg = stage.tile([P, H * PACK], BF16, name="wg", align_bytes=64)
                dst = wg[:].rearrange("p (t m j) -> p m j t", t=PACK, j=PACK)
                src = raw[:].rearrange("p j (m t) -> p m j t", t=PACK)
            engine_copy(item in VECTOR_UNITS, dst, src)
            grouped[item] = wg
            copied["n"] += 1
            load_until(AHEAD + copied["n"])

        accs = {}

        def first_layer(kind, e):
            acc = psum.tile([P, PACK, C], F32, name="acc_" + kind)
            for t in range(PACK):
                for g in range(PASSES):
                    wc, ws = codes[(kind, e, g)]
                    xc, xs = codes[("x", g, e // 2)]
                    sl = slice((e % 2) * C, (e % 2 + 1) * C)
                    nc.tensor.matmul_mx(
                        out=acc[:, t, :],
                        lhsT=wc[:, t * P:(t + 1) * P].bitcast(FP8X4),
                        lhsT_scale=ws[:, t * P:(t + 1) * P],
                        rhs=xc[:, sl].bitcast(FP8X4),
                        rhs_scale=xs[:, sl],
                        start=(g == 0),
                        stop=(g == PASSES - 1),
                    )
            accs[(kind, e)] = acc

        def gelu(e):
            ga = work.tile([P, PACK, C], F32, name="ga")
            nc.scalar.activation(ga[:], accs[("w1", e)][:], GELU)
            accs[("ga", e)] = ga

        def hidden(e):
            hb = work.tile([P, C * PACK], BF16, name="hb", align_bytes=64)
            nc.vector.tensor_tensor(
                out=hb[:].rearrange("p (n t) -> p n t", t=PACK),
                in0=accs[("ga", e)][:].rearrange("p t n -> p n t"),
                in1=accs[("w3", e)][:].rearrange("p t n -> p n t"),
                op=MULT,
            )
            accs[("hb", e)] = hb

        def hidden_quantise(e):
            hq = work.tile([P, C], U32, name="hq", align_bytes=64)
            hs = work.tile([P, C], U8, name="hs", align_bytes=64)
            nc.vector.quantize_mx(out=hq[:].bitcast(FP8X4), scales=hs[:], in_=accs[("hb", e)][:])
            wc, ws = codes[("w2", e, 0)]
            acc_y = psum.tile([P, NT, C], F32, name="acc_y")
            for nt in range(NT):
                nc.tensor.matmul_mx(
                    out=acc_y[:, nt, :],
                    lhsT=wc[:, nt * P:(nt + 1) * P].bitcast(FP8X4),
                    lhsT_scale=ws[:, nt * P:(nt + 1) * P],
                    rhs=hq[:].bitcast(FP8X4),
                    rhs_scale=hs[:],
                    start=True,
                    stop=True,
                )
            accs[("y", e)] = acc_y

        def leave_psum(e):
            ysb = work.tile([P, NT, C], F32, name="ysb")
            nc.scalar.copy(out=ysb[:], in_=accs[("y", e)][:])
            accs[("ysb", e)] = ysb

        windows = [keep.tile([P, T], F32, name="window%d" % nt) for nt in range(NT)]

        def scatter(e, nt):
            nc.vector.tensor_tensor(
                windows[nt][:].indirect(offsets[:, e * (C // 16):(e + 1) * (C // 16)]),
                accs[("ysb", e)][:, nt, :],
                gates[nt][:, e * C:(e + 1) * C],
                MULT,
            )

        for t in range(PACK):
            gather(0, t, 0)
            gather(0, t, 1)
        weight_copy(("w1", 0, 0))
        token_copy(0, 0)
        token_copy(0, 1)
        for t in range(PACK):
            gather(1, t, 0)
            gather(1, t, 1)
        quantise(("x", 0, 0), HALF)
        quantise(("x", 0, 1), HALF)
        weight_copy(("w1", 0, 1))
        token_copy(1, 0)
        token_copy(1, 1)

        last = E - 1
        for e in range(E):
            if e > 0:
                weight_copy(("w1", e, 0))
                hidden(e - 1)
                hidden_quantise(e - 1)
                weight_copy(("w1", e, 1))
                leave_psum(e - 1)
            quantise(("w1", e, 0), H)
            weight_copy(("w3", e, 0))
            if e == 0:
                quantise(("x", 1, 0), HALF)
                quantise(("x", 1, 1), HALF)
            quantise(("w1", e, 1), H)
            first_layer("w1", e)
            if e > 0:
                scatter(e - 1, 0)
                scatter(e - 1, 1)
            if e < last:
                weight_copy(("w2", e, 0))
            gelu(e)
            quantise(("w3", e, 0), H)
            weight_copy(("w3", e, 1))
            if e < last:
                quantise(("w2", e, 0), N)
            else:
                weight_copy(("w2", e, 0))
            quantise(("w3", e, 1), H)
            first_layer("w3", e)

        quantise(("w2", last, 0), N)
        hidden(last)
        hq = work.tile([P, C], U32, name="hq", align_bytes=64)
        hs = work.tile([P, C], U8, name="hs", align_bytes=64)
        nc.vector.quantize_mx(out=hq[:].bitcast(FP8X4), scales=hs[:], in_=accs[("hb", last)][:])
        wc, ws = codes[("w2", last, 0)]
        y_last = []
        for nt in range(NT):
            acc_y = psum.tile([P, C], F32, name="acc_y")
            nc.tensor.matmul_mx(
                out=acc_y[:],
                lhsT=wc[:, nt * P:(nt + 1) * P].bitcast(FP8X4),
                lhsT_scale=ws[:, nt * P:(nt + 1) * P],
                rhs=hq[:].bitcast(FP8X4),
                rhs_scale=hs[:],
                start=True,
                stop=True,
            )
            y_sb = keep.tile([P, C], F32, name="y_last%d" % nt)
            nc.scalar.copy(out=y_sb[:], in_=acc_y[:])
            y_last.append(y_sb)
        for nt in range(NT):
            nc.vector.tensor_tensor(
                windows[nt][:].indirect(offsets[:, last * (C // 16):(last + 1) * (C // 16)]),
                y_last[nt][:],
                gates[nt][:, last * C:(last + 1) * C],
                MULT,
            )
            nc.sync.dma_start(out[nt * P:(nt + 1) * P, :], windows[nt][:])
